import numpy as np
CORES = [24,25,26,27,28,29,30,31,0,8,16]
N = 11
def setup_inputs(rng):
    return {"x": rng.standard_normal((N, 128, 1024), dtype=np.float32)}
def reference(x):
    s = x.max(axis=0)
    return {"y": np.broadcast_to(s, (N,) + s.shape)}

@@ -1,0 +1,158 @@
+from concourse.bass import DstId, RemoteDMATransfer
+
+NG = 2
+G = [26, 27, 30, 31]
+NB = [24, 25, 28, 29]
+RL = [18, 19, 22, 23]
+H0 = [2, 3, 6, 7]
+H1 = [10, 11, 14, 15]
+CHIP3 = [24, 25, 26, 27, 28, 29, 30, 31]
+
+SCRATCH = {
+    "xs": ("dram", [8, 128, 128], "float32"),
+    "ga": ("dram", [17, 128, 128], "float32"),
+    "rb": ("dram", [7, 128, 128], "float32"),
+    "hb": ("dram", [1, 128, 128], "float32"),
+    "pf": ("dram", [4, 128, 128], "float32"),
+    "res": ("dram", [8, 128, 128], "float32"),
+}
+SEMAPHORES = (["s1", "s2", "snt", "sts", "stc"] + ["ld%d" % j for j in range(NG)] + ["r%d" % j for j in range(NG)])
+
+
+def final_core(q, h):
+    return NB[q] if h == 0 else G[q ^ 1]
+
+
+def group_of(q):
+    return q * NG // 4
+
+
+def xfer(srcs, dsts, sem):
+    return {"srcs": srcs, "dsts": dsts, "sem": sem}
+
+
+def build_calls():
+    calls = {}
+
+    def add(core, step, tr):
+        calls.setdefault(core, {}).setdefault(step, []).append(tr)
+
+    for q in range(4):
+        j = group_of(q)
+        for c in CHIP3:
+            if c != G[q]:
+                for h in range(2):
+                    add(c, ("h1", j), xfer([("xs", 2 * q + h)], [(G[q], "ga", 2 * (c - 24) + h)], "s1"))
+        for h in range(2):
+            add(16, ("h1", j), xfer([("xs", 2 * q + h)], [(RL[q], "rb", 2 + h)], "s1"))
+        add(0, ("h1", j), xfer([("xs", 2 * q)], [(RL[q], "rb", 0)], "s1"))
+        add(0, ("h1", j), xfer([("xs", 2 * q + 1)], [(H0[q], "hb", 0)], "s1"))
+        add(8, ("h1", j), xfer([("xs", 2 * q)], [(G[q], "ga", 16)], "s1"))
+        add(8, ("h1", j), xfer([("xs", 2 * q + 1)], [(H1[q], "hb", 0)], "s1"))
+        for h in range(2):
+            srcs = [("xs", 2 * q + h)] + [("ga", 2 * (c - 24) + h) for c in CHIP3 if c != G[q]]
+            if h == 0:
+                srcs.append(("ga", 16))
+            add(G[q], "h2", xfer(srcs, [(RL[q], "rb", 4 + h)], "s2"))
+            add(G[q], "h2", xfer(srcs, [(final_core(q, h), "pf", 0)], "s2"))
+        add(RL[q], "h2", xfer([("rb", 0), ("rb", 2)], [(final_core(q, 0), "pf", 1)], "s2"))
+        add(RL[q], "h2", xfer([("rb", 3)], [(final_core(q, 1), "pf", 1)], "s2"))
+        add(H0[q], "h2", xfer([("hb", 0)], [(RL[q], "rb", 1), (final_core(q, 1), "pf", 2)], "s2"))
+        add(H1[q], "h2", xfer([("hb", 0)], [(RL[q], "rb", 6), (final_core(q, 1), "pf", 3)], "s2"))
+        for h in range(2):
+            e = 2 * q + h
+            f = final_core(q, h)
+            sem = "r%d" % j
+            srcs = [("pf", k) for k in range(2 if h == 0 else 4)]
+            others = [c for c in CHIP3 if c != f]
+            add(f, "h3", xfer(srcs, [(c, "res", e) for c in [8] + others[:3]], sem))
+            add(f, "h3", xfer(srcs, [(c, "res", e) for c in others[3:]], sem))
+            srcs = [("rb", h), ("rb", 2 + h), ("rb", 4 + h)] + ([("rb", 6)] if h == 1 else [])
+            add(RL[q], "h3", xfer(srcs, [(0, "res", e), (f, "res", e)], sem))
+            add(RL[q], "h3", xfer(srcs, [(16, "res", e)], sem))
+    for core in calls:
+        for step in calls[core]:
+            trs = calls[core][step]
+            off = [t for t in trs if any(d[0] // 8 != core // 8 for d in t["dsts"])]
+            on = [t for t in trs if not any(d[0] // 8 != core // 8 for d in t["dsts"])]
+            room_on = 16 if not off else 8
+            lo, hi = 0, 16
+            for cls, room in ((off, 8), (on, room_on)):
+                if not cls:
+                    continue
+                n = 1
+                while n * 2 * len(cls) <= room:
+                    n *= 2
+                for t in cls:
+                    if cls is off:
+                        t["mask"] = ((1 << n) - 1) << lo
+                        lo += n
+                    else:
+                        hi -= n
+                        t["mask"] = ((1 << n) - 1) << hi
+                    t["n"] = n
+            assert lo <= hi and lo <= 8
+    return calls
+
+
+def arrivals(calls):
+    inc = {}
+    for core in calls:
+        for step in calls[core]:
+            for t in calls[core][step]:
+                for d in t["dsts"]:
+                    inc[(d[0], t["sem"])] = inc.get((d[0], t["sem"]), 0) + t["n"]
+    return inc
+
+
+def rank_program(g, core, T, topo):
+    calls = build_calls()
+    inc = arrivals(calls)
+    mine = calls.get(core, {})
+    is_rank = T.rank_of(core) is not None
+    sent = [0]
+
+    def issue(step):
+        trs = []
+        for t in mine[step]:
+            where = []
+            for d in t["dsts"]:
+                a = topo.addr(d[0])
+                where.append(DstId(rid=a[0], pnc=a[1]))
+            trs.append(RemoteDMATransfer(
+                dst_ids=where, dma_engine_mask=t["mask"], remote_sem=T.sem[t["sem"]],
+                srcs=[T[b][s] for (b, s) in t["srcs"]], dsts=[T[d[1]][d[2]] for d in t["dsts"]],
+                alu_op=2 if len(t["srcs"]) > 1 else 0))
+            sent[0] += t["n"]
+        g.remote_dma_fused(trs, local_sem=T.sem.snt)
+
+    per = 8 // NG
+    queues = [g.sync, g.scalar]
+    if is_rank:
+        for j in range(NG):
+            a, b = j * per, (j + 1) * per
+            queues[j % 2].dma_start(T.xs[a:b], T.x[16 * a:16 * b, :]).then_inc(T.sem["ld%d" % j], 16)
+        for j in range(NG):
+            g.wait_ge(T.sem["ld%d" % j], 16)
+            if ("h1", j) in mine:
+                issue(("h1", j))
+    if "h2" in mine:
+        g.wait_ge(T.sem.s1, inc[(core, "s1")])
+        issue("h2")
+    if "h3" in mine:
+        g.wait_ge(T.sem.s2, inc[(core, "s2")])
+        issue("h3")
+    if is_rank:
+        nst = [0, 0]
+        for j in range(NG):
+            a, b = j * per, (j + 1) * per
+            qu = queues[j % 2]
+            qu.wait_ge(T.sem["r%d" % j], inc[(core, "r%d" % j)])
+            qu.dma_start(T.y[16 * a:16 * b, :], T.res[a:b]).then_inc(T.sem.sts if j % 2 == 0 else T.sem.stc, 16)
+            nst[j % 2] += 16
+        if nst[0]:
+            g.sync.wait_ge(T.sem.sts, nst[0])
+        if nst[1]:
+            g.scalar.wait_ge(T.sem.stc, nst[1])
+    if sent[0]:
+        g.wait_ge(T.sem.snt, sent[0])

@@ -10,25 +10,29 @@ CHIP3 = [24, 25, 26, 27, 28, 29, 30, 31]
 
 SCRATCH = {
     "xs": ("dram", [8, 128, 128], "float32"),
-    "ga": ("dram", [17, 128, 128], "float32"),
-    "rb": ("dram", [7, 128, 128], "float32"),
+    "ga": ("dram", [9, 128, 128], "float32"),
+    "rb": ("dram", [4, 128, 128], "float32"),
     "hb": ("dram", [1, 128, 128], "float32"),
     "pf": ("dram", [4, 128, 128], "float32"),
     "res": ("dram", [8, 128, 128], "float32"),
 }
-SEMAPHORES = (["s1", "s2", "snt", "sts", "stc"] + ["ld%d" % j for j in range(NG)] + ["r%d" % j for j in range(NG)])
+SEMAPHORES = (["s1", "s2", "s3", "snt", "sts", "stc"] + ["ld%d" % j for j in range(NG)] + ["r%d" % j for j in range(NG)])
+
+
+def gather_core(q, h):
+    return NB[q] if h == 0 else G[q]
 
 
 def final_core(q, h):
-    return NB[q] if h == 0 else G[q ^ 1]
+    return NB[q ^ 1] if h == 0 else G[q ^ 1]
 
 
 def group_of(q):
     return q * NG // 4
 
 
-def xfer(srcs, dsts, sem):
-    return {"srcs": srcs, "dsts": dsts, "sem": sem}
+def xfer(srcs, dsts, sem, lo=-1, n=0):
+    return {"srcs": srcs, "dsts": dsts, "sem": sem, "lo": lo, "n": n}
 
 
 def build_calls():
@@ -39,59 +43,51 @@ def build_calls():
 
     for q in range(4):
         j = group_of(q)
-        for c in CHIP3:
-            if c != G[q]:
-                for h in range(2):
-                    add(c, ("h1", j), xfer([("xs", 2 * q + h)], [(G[q], "ga", 2 * (c - 24) + h)], "s1"))
-        for h in range(2):
-            add(16, ("h1", j), xfer([("xs", 2 * q + h)], [(RL[q], "rb", 2 + h)], "s1"))
-        add(0, ("h1", j), xfer([("xs", 2 * q)], [(RL[q], "rb", 0)], "s1"))
-        add(0, ("h1", j), xfer([("xs", 2 * q + 1)], [(H0[q], "hb", 0)], "s1"))
-        add(8, ("h1", j), xfer([("xs", 2 * q)], [(G[q], "ga", 16)], "s1"))
-        add(8, ("h1", j), xfer([("xs", 2 * q + 1)], [(H1[q], "hb", 0)], "s1"))
-        for h in range(2):
-            srcs = [("xs", 2 * q + h)] + [("ga", 2 * (c - 24) + h) for c in CHIP3 if c != G[q]]
-            if h == 0:
-                srcs.append(("ga", 16))
-            add(G[q], "h2", xfer(srcs, [(RL[q], "rb", 4 + h)], "s2"))
-            add(G[q], "h2", xfer(srcs, [(final_core(q, h), "pf", 0)], "s2"))
-        add(RL[q], "h2", xfer([("rb", 0), ("rb", 2)], [(final_core(q, 0), "pf", 1)], "s2"))
-        add(RL[q], "h2", xfer([("rb", 3)], [(final_core(q, 1), "pf", 1)], "s2"))
-        add(H0[q], "h2", xfer([("hb", 0)], [(RL[q], "rb", 1), (final_core(q, 1), "pf", 2)], "s2"))
-        add(H1[q], "h2", xfer([("hb", 0)], [(RL[q], "rb", 6), (final_core(q, 1), "pf", 3)], "s2"))
+        rsem = "r%d" % j
         for h in range(2):
             e = 2 * q + h
+            k = gather_core(q, h)
             f = final_core(q, h)
-            sem = "r%d" % j
-            srcs = [("pf", k) for k in range(2 if h == 0 else 4)]
-            others = [c for c in CHIP3 if c != f]
-            add(f, "h3", xfer(srcs, [(c, "res", e) for c in [8] + others[:3]], sem))
-            add(f, "h3", xfer(srcs, [(c, "res", e) for c in others[3:]], sem))
-            srcs = [("rb", h), ("rb", 2 + h), ("rb", 4 + h)] + ([("rb", 6)] if h == 1 else [])
-            add(RL[q], "h3", xfer(srcs, [(0, "res", e), (f, "res", e)], sem))
-            add(RL[q], "h3", xfer(srcs, [(16, "res", e)], sem))
+            for c in CHIP3:
+                if c != k:
+                    add(c, ("h1", j), xfer([("xs", e)], [(k, "ga", c - 24)], "s1"))
+            add(16, ("h1", j), xfer([("xs", e)], [(RL[q], "rb", 2 + h)], "s1"))
+            add(0, ("h1", j), xfer([("xs", e)], [(RL[q], "rb", 0) if h == 0 else (H0[q], "hb", 0)], "s1"))
+            add(8, ("h1", j), xfer([("xs", e)], [(k, "ga", 8) if h == 0 else (H1[q], "hb", 0)], "s1"))
+            srcs = [("xs", e)] + [("ga", c - 24) for c in CHIP3 if c != k] + ([("ga", 8)] if h == 0 else [])
+            add(k, "h2", xfer(srcs, [(f, "pf", 0)], "s2"))
+            add(RL[q], "h2", xfer([("rb", 0), ("rb", 2)] if h == 0 else [("rb", 3)], [(f, "pf", 1)], "s2"))
+            if h == 1:
+                add(H0[q], "h2", xfer([("hb", 0)], [(f, "pf", 2)], "s2"))
+                add(H1[q], "h2", xfer([("hb", 0)], [(f, "pf", 3)], "s2"))
+            add(f, "h3", xfer([("pf", i) for i in range(2 if h == 0 else 4)], [(G[q], "res", e), (NB[q], "res", e)], "s3"))
+            rest = [c for c in CHIP3 if c != G[q] and c != NB[q]]
+            add(G[q], "h4", xfer([("res", e)], [(16, "res", e), (0, "res", e)], rsem, 4 * h, 4))
+            add(NB[q], "h4", xfer([("res", e)], [(8, "res", e), (rest[5], "res", e)], rsem, 4 * h, 4))
+            add(G[q] if h == 0 else NB[q], "h4", xfer([("res", e)], [(c, "res", e) for c in rest[:5]], rsem, 8, 8))
     for core in calls:
         for step in calls[core]:
             trs = calls[core][step]
             off = [t for t in trs if any(d[0] // 8 != core // 8 for d in t["dsts"])]
             on = [t for t in trs if not any(d[0] // 8 != core // 8 for d in t["dsts"])]
-            room_on = 16 if not off else 8
             lo, hi = 0, 16
-            for cls, room in ((off, 8), (on, room_on)):
-                if not cls:
-                    continue
+            for cls, room in ((off, 8), (on, 16 if not off else 8)):
                 n = 1
-                while n * 2 * len(cls) <= room:
+                while cls and n * 2 * len(cls) <= room:
                     n *= 2
                 for t in cls:
+                    if t["n"]:
+                        continue
+                    t["n"] = n
                     if cls is off:
-                        t["mask"] = ((1 << n) - 1) << lo
+                        t["lo"] = lo
                         lo += n
                     else:
                         hi -= n
-                        t["mask"] = ((1 << n) - 1) << hi
-                    t["n"] = n
+                        t["lo"] = hi
             assert lo <= hi and lo <= 8
+            for t in trs:
+                t["mask"] = ((1 << t["n"]) - 1) << t["lo"]
     return calls
 
 
@@ -136,18 +132,20 @@ def rank_program(g, core, T, topo):
             g.wait_ge(T.sem["ld%d" % j], 16)
             if ("h1", j) in mine:
                 issue(("h1", j))
-    if "h2" in mine:
-        g.wait_ge(T.sem.s1, inc[(core, "s1")])
-        issue("h2")
-    if "h3" in mine:
-        g.wait_ge(T.sem.s2, inc[(core, "s2")])
-        issue("h3")
+    for step, sem in (("h2", "s1"), ("h3", "s2"), ("h4", "s3")):
+        if step in mine:
+            g.wait_ge(T.sem[sem], inc[(core, sem)])
+            issue(step)
     if is_rank:
+        own = [group_of(q) for q in range(4) if core == G[q] or core == NB[q]]
         nst = [0, 0]
         for j in range(NG):
             a, b = j * per, (j + 1) * per
             qu = queues[j % 2]
-            qu.wait_ge(T.sem["r%d" % j], inc[(core, "r%d" % j)])
+            if j in own:
+                qu.wait_ge(T.sem.s3, inc[(core, "s3")])
+            if (core, "r%d" % j) in inc:
+                qu.wait_ge(T.sem["r%d" % j], inc[(core, "r%d" % j)])
             qu.dma_start(T.y[16 * a:16 * b, :], T.res[a:b]).then_inc(T.sem.sts if j % 2 == 0 else T.sem.stc, 16)
             nst[j % 2] += 16
         if nst[0]:

@@ -1,6 +1,8 @@
 from concourse.bass import DstId, RemoteDMATransfer
 
-NG = 2
+NP = 2
+W = 128 // NP
+RP = 16 // NP
 G = [26, 27, 30, 31]
 NB = [24, 25, 28, 29]
 RL = [18, 19, 22, 23]
@@ -9,14 +11,14 @@ H1 = [10, 11, 14, 15]
 CHIP3 = [24, 25, 26, 27, 28, 29, 30, 31]
 
 SCRATCH = {
-    "xs": ("dram", [8, 128, 128], "float32"),
-    "ga": ("dram", [9, 128, 128], "float32"),
-    "rb": ("dram", [4, 128, 128], "float32"),
-    "hb": ("dram", [1, 128, 128], "float32"),
-    "pf": ("dram", [4, 128, 128], "float32"),
-    "res": ("dram", [8, 128, 128], "float32"),
+    "xs": ("dram", [8 * NP, 128, W], "float32"),
+    "ga": ("dram", [9 * NP, 128, W], "float32"),
+    "rb": ("dram", [4 * NP, 128, W], "float32"),
+    "hb": ("dram", [NP, 128, W], "float32"),
+    "pf": ("dram", [4 * NP, 128, W], "float32"),
+    "res": ("dram", [8 * NP, 128, W], "float32"),
 }
-SEMAPHORES = (["s1", "s2", "s3", "snt", "sts", "stc"] + ["ld%d" % j for j in range(NG)] + ["r%d" % j for j in range(NG)])
+SEMAPHORES = ["snt", "sts", "stc"] + ["%s%d" % (s, p) for s in ("ld", "a", "b", "c", "r") for p in range(NP)]
 
 
 def gather_core(q, h):
@@ -25,10 +27,6 @@ def gather_core(q, h):
 
 def final_core(q, h):
     return NB[q ^ 1] if h == 0 else G[q ^ 1]
-
-
-def group_of(q):
-    return q * NG // 4
 
 
 def xfer(srcs, dsts, sem, lo=-1, n=0):
@@ -41,30 +39,34 @@ def build_calls():
     def add(core, step, tr):
         calls.setdefault(core, {}).setdefault(step, []).append(tr)
 
-    for q in range(4):
-        j = group_of(q)
-        rsem = "r%d" % j
-        for h in range(2):
-            e = 2 * q + h
-            k = gather_core(q, h)
-            f = final_core(q, h)
-            for c in CHIP3:
-                if c != k:
-                    add(c, ("h1", j), xfer([("xs", e)], [(k, "ga", c - 24)], "s1"))
-            add(16, ("h1", j), xfer([("xs", e)], [(RL[q], "rb", 2 + h)], "s1"))
-            add(0, ("h1", j), xfer([("xs", e)], [(RL[q], "rb", 0) if h == 0 else (H0[q], "hb", 0)], "s1"))
-            add(8, ("h1", j), xfer([("xs", e)], [(k, "ga", 8) if h == 0 else (H1[q], "hb", 0)], "s1"))
-            srcs = [("xs", e)] + [("ga", c - 24) for c in CHIP3 if c != k] + ([("ga", 8)] if h == 0 else [])
-            add(k, "h2", xfer(srcs, [(f, "pf", 0)], "s2"))
-            add(RL[q], "h2", xfer([("rb", 0), ("rb", 2)] if h == 0 else [("rb", 3)], [(f, "pf", 1)], "s2"))
-            if h == 1:
-                add(H0[q], "h2", xfer([("hb", 0)], [(f, "pf", 2)], "s2"))
-                add(H1[q], "h2", xfer([("hb", 0)], [(f, "pf", 3)], "s2"))
-            add(f, "h3", xfer([("pf", i) for i in range(2 if h == 0 else 4)], [(G[q], "res", e), (NB[q], "res", e)], "s3"))
-            rest = [c for c in CHIP3 if c != G[q] and c != NB[q]]
-            add(G[q], "h4", xfer([("res", e)], [(16, "res", e), (0, "res", e)], rsem, 4 * h, 4))
-            add(NB[q], "h4", xfer([("res", e)], [(8, "res", e), (rest[5], "res", e)], rsem, 4 * h, 4))
-            add(G[q] if h == 0 else NB[q], "h4", xfer([("res", e)], [(c, "res", e) for c in rest[:5]], rsem, 8, 8))
+    for p in range(NP):
+        sa, sb, sc, sr = "a%d" % p, "b%d" % p, "c%d" % p, "r%d" % p
+        for q in range(4):
+            for h in range(2):
+                e = 8 * p + 2 * q + h
+                k = gather_core(q, h)
+                f = final_core(q, h)
+                for c in CHIP3:
+                    if c != k:
+                        add(c, (1, p), xfer([("xs", e)], [(k, "ga", 9 * p + c - 24)], sa))
+                add(16, (1, p), xfer([("xs", e)], [(RL[q], "rb", 4 * p + 2 + h)], sa))
+                add(0, (1, p), xfer([("xs", e)], [(RL[q], "rb", 4 * p) if h == 0 else (H0[q], "hb", p)], sa))
+                add(8, (1, p), xfer([("xs", e)], [(k, "ga", 9 * p + 8) if h == 0 else (H1[q], "hb", p)], sa))
+                srcs = [("xs", e)] + [("ga", 9 * p + c - 24) for c in CHIP3 if c != k]
+                if h == 0:
+                    srcs.append(("ga", 9 * p + 8))
+                add(k, (2, p), xfer(srcs, [(f, "pf", 4 * p)], sb))
+                srcs = [("rb", 4 * p), ("rb", 4 * p + 2)] if h == 0 else [("rb", 4 * p + 3)]
+                add(RL[q], (2, p), xfer(srcs, [(f, "pf", 4 * p + 1)], sb))
+                if h == 1:
+                    add(H0[q], (2, p), xfer([("hb", p)], [(f, "pf", 4 * p + 2)], sb))
+                    add(H1[q], (2, p), xfer([("hb", p)], [(f, "pf", 4 * p + 3)], sb))
+                srcs = [("pf", 4 * p + i) for i in range(2 if h == 0 else 4)]
+                add(f, (3, p), xfer(srcs, [(G[q], "res", e), (NB[q], "res", e)], sc))
+                rest = [c for c in CHIP3 if c != G[q] and c != NB[q]]
+                add(G[q], (4, p), xfer([("res", e)], [(16, "res", e), (0, "res", e)], sr, 4 * h, 4))
+                add(NB[q], (4, p), xfer([("res", e)], [(8, "res", e), (rest[5], "res", e)], sr, 4 * h, 4))
+                add(G[q] if h == 0 else NB[q], (4, p), xfer([("res", e)], [(c, "res", e) for c in rest[:5]], sr, 8, 8))
     for core in calls:
         for step in calls[core]:
             trs = calls[core][step]
@@ -122,32 +124,28 @@ def rank_program(g, core, T, topo):
             sent[0] += t["n"]
         g.remote_dma_fused(trs, local_sem=T.sem.snt)
 
-    per = 8 // NG
     queues = [g.sync, g.scalar]
     if is_rank:
-        for j in range(NG):
-            a, b = j * per, (j + 1) * per
-            queues[j % 2].dma_start(T.xs[a:b], T.x[16 * a:16 * b, :]).then_inc(T.sem["ld%d" % j], 16)
-        for j in range(NG):
-            g.wait_ge(T.sem["ld%d" % j], 16)
-            if ("h1", j) in mine:
-                issue(("h1", j))
-    for step, sem in (("h2", "s1"), ("h3", "s2"), ("h4", "s3")):
-        if step in mine:
-            g.wait_ge(T.sem[sem], inc[(core, sem)])
-            issue(step)
+        for p in range(NP):
+            queues[p % 2].dma_start(T.xs[8 * p:8 * p + 8], T.x[8 * RP * p:8 * RP * (p + 1), :]).then_inc(T.sem["ld%d" % p], 16)
+        for p in range(NP):
+            g.wait_ge(T.sem["ld%d" % p], 16)
+            issue((1, p))
+    for hop, sem in ((2, "a"), (3, "b"), (4, "c")):
+        for p in range(NP):
+            if (hop, p) in mine:
+                g.wait_ge(T.sem["%s%d" % (sem, p)], inc[(core, "%s%d" % (sem, p))])
+                issue((hop, p))
     if is_rank:
-        own = [group_of(q) for q in range(4) if core == G[q] or core == NB[q]]
         nst = [0, 0]
-        for j in range(NG):
-            a, b = j * per, (j + 1) * per
-            qu = queues[j % 2]
-            if j in own:
-                qu.wait_ge(T.sem.s3, inc[(core, "s3")])
-            if (core, "r%d" % j) in inc:
-                qu.wait_ge(T.sem["r%d" % j], inc[(core, "r%d" % j)])
-            qu.dma_start(T.y[16 * a:16 * b, :], T.res[a:b]).then_inc(T.sem.sts if j % 2 == 0 else T.sem.stc, 16)
-            nst[j % 2] += 16
+        for p in range(NP):
+            qu = queues[p % 2]
+            if (core, "c%d" % p) in inc:
+                qu.wait_ge(T.sem["c%d" % p], inc[(core, "c%d" % p)])
+            qu.wait_ge(T.sem["r%d" % p], inc[(core, "r%d" % p)])
+            qu.dma_start(T.y[8 * RP * p:8 * RP * (p + 1), :], T.res[8 * p:8 * p + 8]).then_inc(
+                T.sem.sts if p % 2 == 0 else T.sem.stc, 16)
+            nst[p % 2] += 16
         if nst[0]:
             g.sync.wait_ge(T.sem.sts, nst[0])
         if nst[1]:

from concourse.bass import DstId, RemoteDMATransfer

NP = 2
W = 128 // NP
RP = 16 // NP
G = [26, 27, 30, 31]
NB = [24, 25, 28, 29]
RL = [18, 19, 22, 23]
H0 = [2, 3, 6, 7]
H1 = [10, 11, 14, 15]
CHIP3 = [24, 25, 26, 27, 28, 29, 30, 31]

SCRATCH = {
    "xs": ("dram", [8 * NP, 128, W], "float32"),
    "ga": ("dram", [9 * NP, 128, W], "float32"),
    "rb": ("dram", [4 * NP, 128, W], "float32"),
    "hb": ("dram", [NP, 128, W], "float32"),
    "pf": ("dram", [4 * NP, 128, W], "float32"),
    "res": ("dram", [8 * NP, 128, W], "float32"),
}
SEMAPHORES = ["snt", "sts", "stc"] + ["%s%d" % (s, p) for s in ("ld", "a", "b", "c", "r") for p in range(NP)]


def gather_core(q, h):
    return NB[q] if h == 0 else G[q]


def final_core(q, h):
    return NB[q ^ 1] if h == 0 else G[q ^ 1]


def xfer(srcs, dsts, sem, lo=-1, n=0):
    return {"srcs": srcs, "dsts": dsts, "sem": sem, "lo": lo, "n": n}


def build_calls():
    calls = {}

    def add(core, step, tr):
        calls.setdefault(core, {}).setdefault(step, []).append(tr)

    for p in range(NP):
        sa, sb, sc, sr = "a%d" % p, "b%d" % p, "c%d" % p, "r%d" % p
        for q in range(4):
            for h in range(2):
                e = 8 * p + 2 * q + h
                k = gather_core(q, h)
                f = final_core(q, h)
                for c in CHIP3:
                    if c != k:
                        add(c, (1, p), xfer([("xs", e)], [(k, "ga", 9 * p + c - 24)], sa))
                add(16, (1, p), xfer([("xs", e)], [(RL[q], "rb", 4 * p + 2 + h)], sa))
                add(0, (1, p), xfer([("xs", e)], [(RL[q], "rb", 4 * p) if h == 0 else (H0[q], "hb", p)], sa))
                add(8, (1, p), xfer([("xs", e)], [(k, "ga", 9 * p + 8) if h == 0 else (H1[q], "hb", p)], sa))
                srcs = [("xs", e)] + [("ga", 9 * p + c - 24) for c in CHIP3 if c != k]
                if h == 0:
                    srcs.append(("ga", 9 * p + 8))
                add(k, (2, p), xfer(srcs, [(f, "pf", 4 * p)], sb))
                srcs = [("rb", 4 * p), ("rb", 4 * p + 2)] if h == 0 else [("rb", 4 * p + 3)]
                add(RL[q], (2, p), xfer(srcs, [(f, "pf", 4 * p + 1)], sb))
                if h == 1:
                    add(H0[q], (2, p), xfer([("hb", p)], [(f, "pf", 4 * p + 2)], sb))
                    add(H1[q], (2, p), xfer([("hb", p)], [(f, "pf", 4 * p + 3)], sb))
                srcs = [("pf", 4 * p + i) for i in range(2 if h == 0 else 4)]
                add(f, (3, p), xfer(srcs, [(G[q], "res", e), (NB[q], "res", e)], sc))
                rest = [c for c in CHIP3 if c != G[q] and c != NB[q]]
                add(G[q], (4, p), xfer([("res", e)], [(16, "res", e), (0, "res", e)], sr, 4 * h, 4))
                add(NB[q], (4, p), xfer([("res", e)], [(8, "res", e), (rest[5], "res", e)], sr, 4 * h, 4))
                add(G[q] if h == 0 else NB[q], (4, p), xfer([("res", e)], [(c, "res", e) for c in rest[:5]], sr, 8, 8))
    for core in calls:
        for step in calls[core]:
            trs = calls[core][step]
            off = [t for t in trs if any(d[0] // 8 != core // 8 for d in t["dsts"])]
            on = [t for t in trs if not any(d[0] // 8 != core // 8 for d in t["dsts"])]
            lo, hi = 0, 16
            for cls, room in ((off, 8), (on, 16 if not off else 8)):
                n = 1
                while cls and n * 2 * len(cls) <= room:
                    n *= 2
                for t in cls:
                    if t["n"]:
                        continue
                    t["n"] = n
                    if cls is off:
                        t["lo"] = lo
                        lo += n
                    else:
                        hi -= n
                        t["lo"] = hi
            assert lo <= hi and lo <= 8
            for t in trs:
                t["mask"] = ((1 << t["n"]) - 1) << t["lo"]
    return calls


def arrivals(calls):
    inc = {}
    for core in calls:
        for step in calls[core]:
            for t in calls[core][step]:
                for d in t["dsts"]:
                    inc[(d[0], t["sem"])] = inc.get((d[0], t["sem"]), 0) + t["n"]
    return inc


def rank_program(g, core, T, topo):
    calls = build_calls()
    inc = arrivals(calls)
    mine = calls.get(core, {})
    is_rank = T.rank_of(core) is not None
    sent = [0]

    def issue(step):
        trs = []
        for t in mine[step]:
            where = []
            for d in t["dsts"]:
                a = topo.addr(d[0])
                where.append(DstId(rid=a[0], pnc=a[1]))
            trs.append(RemoteDMATransfer(
                dst_ids=where, dma_engine_mask=t["mask"], remote_sem=T.sem[t["sem"]],
                srcs=[T[b][s] for (b, s) in t["srcs"]], dsts=[T[d[1]][d[2]] for d in t["dsts"]],
                alu_op=2 if len(t["srcs"]) > 1 else 0))
            sent[0] += t["n"]
        g.remote_dma_fused(trs, local_sem=T.sem.snt)

    queues = [g.sync, g.scalar]
    if is_rank:
        for p in range(NP):
            queues[p % 2].dma_start(T.xs[8 * p:8 * p + 8], T.x[8 * RP * p:8 * RP * (p + 1), :]).then_inc(T.sem["ld%d" % p], 16)
        for p in range(NP):
            g.wait_ge(T.sem["ld%d" % p], 16)
            issue((1, p))
    for hop, sem in ((2, "a"), (3, "b"), (4, "c")):
        for p in range(NP):
            if (hop, p) in mine:
                g.wait_ge(T.sem["%s%d" % (sem, p)], inc[(core, "%s%d" % (sem, p))])
                issue((hop, p))
    if is_rank:
        nst = [0, 0]
        for p in range(NP):
            qu = queues[p % 2]
            if (core, "c%d" % p) in inc:
                qu.wait_ge(T.sem["c%d" % p], inc[(core, "c%d" % p)])
            qu.wait_ge(T.sem["r%d" % p], inc[(core, "r%d" % p)])
            qu.dma_start(T.y[8 * RP * p:8 * RP * (p + 1), :], T.res[8 * p:8 * p + 8]).then_inc(
                T.sem.sts if p % 2 == 0 else T.sem.stc, 16)
            nst[p % 2] += 16
        if nst[0]:
            g.sync.wait_ge(T.sem.sts, nst[0])
        if nst[1]:
            g.scalar.wait_ge(T.sem.stc, nst[1])
    if sent[0]:
        g.wait_ge(T.sem.snt, sent[0])
